import numpy as np
import ml_dtypes


def mxq(x, axis, fmt="e4m3"):
    dtype, down = {"e4m3": (ml_dtypes.float8_e4m3fn, 7), "e5m2": (ml_dtypes.float8_e5m2, 14)}[fmt]
    v = np.moveaxis(np.asarray(x, np.float32).astype(ml_dtypes.bfloat16).astype(np.float64), axis, -1)
    blocks = v.reshape(v.shape[:-1] + (-1, 32))
    amax = np.abs(blocks).max(-1, keepdims=True)
    byte = np.maximum(np.where(amax > 0, np.frexp(amax)[1] - 1 + 127, 0) - down, 1)
    scale = np.exp2(byte - 127.0)
    codes = (blocks / scale).astype(np.float32).astype(dtype).astype(np.float64)
    return np.moveaxis((codes * scale).reshape(v.shape), -1, axis)


WIDE = False


def mx_kscale(k):
    if not WIDE:
        return np.ones(k)
    levels = np.array([10, -10, 5, -5, 0])
    if k % 512:
        return np.exp2(np.random.permutation(np.resize(levels, k // 32))).repeat(32)
    a = np.empty((k // 512, 16))
    for p in range(k // 512):
        a[p, :8] = np.random.permutation(np.resize(levels, 8))
        for g in range(8):
            far = levels[np.abs(levels - a[p, g]) >= 10]
            a[p, g + 8] = far[np.random.randint(len(far))]
    return np.exp2(a.ravel()).repeat(32)


def f64(x):
    return np.asarray(x).astype(np.float64)


def striped(idx):
    return np.tile(np.asarray(idx).reshape(-1, 16).T, (8, 1)).astype(np.uint16)


def unstriped(offs):
    return offs[:16].T.reshape(-1).astype(np.int64)


B, N, T, D, DV, NQ = 1, 512, 1024, 256, 0, 512


def setup_inputs():
    n = np.random.standard_normal
    idx = np.random.permutation(T)[:B * N]
    z = mx_kscale(NQ)[:, None]
    return {
        "g": (n((B, NQ, N)) * z / np.sqrt(NQ)).astype(np.float32),
        "qm": (n((B, NQ, D)) / z).astype(np.float32),
        "offs": striped(idx),
    }


def reference(g, qm, offs):
    idx = unstriped(offs)
    dk = mxq(f64(qm), 1, "e4m3").transpose(0, 2, 1) @ mxq(f64(g), 1, "e4m3")
    out = np.zeros((D, T))
    out[:, idx] = dk.transpose(1, 0, 2).reshape(D, B * N)
    return out

@@ -1,0 +1,103 @@
+from contextlib import ExitStack
+
+import concourse.mybir as mybir
+
+F32 = mybir.dt.float32
+BF16 = mybir.dt.bfloat16
+U32 = mybir.dt.uint32
+U16 = mybir.dt.uint16
+U8 = mybir.dt.uint8
+FP8X4 = mybir.dt.float8_e4m3fn_x4
+
+P = 128
+PACK = 4
+NQ = 512
+SLOTS = 512
+D = 256
+T = 1024
+BLOCKS = D // P
+
+FLOPS = 2 * NQ * SLOTS * D
+
+CHUNKS = [128,128,256]
+
+
+def interleave(nc, grouped, raw, vector_cols, width):
+    for copy, a, b in ((nc.vector.tensor_copy, 0, vector_cols), (nc.scalar.copy, vector_cols, width)):
+        if b > a:
+            copy(
+                out=grouped[:, a:b, :].rearrange("p (c i) t -> p c t i", i=4),
+                in_=raw[:, :, a:b].rearrange("p t (c i) -> p c t i", i=4),
+            )
+
+
+def quantise(nc, codes, scales, grouped):
+    nc.vector.quantize_mx(
+        out=codes[:].bitcast(FP8X4),
+        scales=scales[:],
+        in_=grouped[:].rearrange("p c t -> p (c t)"),
+    )
+
+
+def tile_attend_dk_kernel(tc, g, qm, offs, out):
+    nc = tc.nc
+    g_rows = g.rearrange("b (p t) n -> p (b t) n", t=PACK)
+    qm_rows = qm.rearrange("b (p t) d -> p (b t) d", t=PACK)
+    starts = [sum(CHUNKS[:c]) for c in range(len(CHUNKS))]
+
+    with ExitStack() as ctx:
+        held = ctx.enter_context(tc.tile_pool(name="held", bufs=1))
+        psum = ctx.enter_context(tc.psum_pool(name="psum", bufs=1))
+
+        offsets = held.tile([P, SLOTS // 16], U16, name="offsets")
+        qm_raw = held.tile([P, PACK, D], F32, name="qm_raw")
+        g_raw = [held.tile([P, PACK, w], F32, name=f"g_raw{c}") for c, w in enumerate(CHUNKS)]
+        warm = held.tile([P, 8], F32, name="warm")
+
+        nc.sync.dma_start(out=qm_raw[:], in_=qm_rows)
+        for c, w in enumerate(CHUNKS):
+            nc.sync.dma_start(out=g_raw[c][:], in_=g_rows[:, :, starts[c] : starts[c] + w])
+            if c == 0:
+                nc.sync.dma_start(offsets[:], offs)
+
+        windows = [held.tile([P, T], F32, name=f"window{b}") for b in range(BLOCKS)]
+        nc.vector.memset(warm[:], 0.0)
+        nc.scalar.copy(out=warm[:, 4:8], in_=warm[:, 0:4])
+        nc.vector.memset(windows[0][:], 0.0)
+        nc.gpsimd.memset(windows[1][:], 0.0)
+
+        qm_grouped = held.tile([P, D, PACK], BF16, name="qm_grouped", align_bytes=64)
+        qm_codes = held.tile([P, D], U32, name="qm_codes", align_bytes=64)
+        qm_scales = held.tile([P, D], U8, name="qm_scales", align_bytes=64)
+        interleave(nc, qm_grouped, qm_raw, 176, D)
+        quantise(nc, qm_codes, qm_scales, qm_grouped)
+
+        g_codes, g_scales, staged = [], [], []
+        for c, w in enumerate(CHUNKS):
+            grouped = held.tile([P, w, PACK], BF16, name=f"g_grouped{c}", align_bytes=64)
+            g_codes.append(held.tile([P, w], U32, name=f"g_codes{c}", align_bytes=64))
+            g_scales.append(held.tile([P, w], U8, name=f"g_scales{c}", align_bytes=64))
+            interleave(nc, grouped, g_raw[c], int(w * 0.69) // 8 * 8, w)
+            quantise(nc, g_codes[c], g_scales[c], grouped)
+
+            for b in range(BLOCKS):
+                rows = slice(b * P, (b + 1) * P)
+                acc = psum.tile([P, w], F32, name=f"acc{c}_{b}")
+                nc.tensor.matmul_mx(
+                    out=acc[:],
+                    lhsT=qm_codes[:, rows].bitcast(FP8X4),
+                    lhsT_scale=qm_scales[:, rows],
+                    rhs=g_codes[c][:].bitcast(FP8X4),
+                    rhs_scale=g_scales[c][:],
+                    start=True,
+                    stop=True,
+                )
+                values = held.tile([P, w], F32, name=f"values{c}_{b}")
+                nc.scalar.copy(out=values[:], in_=acc[:])
+                staged.append((b, c, values))
+
+        for b, c, values in sorted(staged, key=lambda s: s[0] * 10 + s[1]):
+            listed = offsets[:, starts[c] // 16 : (starts[c] + CHUNKS[c]) // 16]
+            nc.vector.tensor_copy(windows[b][:].indirect(listed), values[:])
+        for b in range(BLOCKS):
+            nc.sync.dma_start(out=out[b * P : (b + 1) * P, :], in_=windows[b][:])

@@ -19,6 +19,7 @@ BLOCKS = D // P
 
 FLOPS = 2 * NQ * SLOTS * D
 
+
 CHUNKS = [128,128,256]
 
 
@@ -31,73 +32,86 @@ def interleave(nc, grouped, raw, vector_cols, width):
             )
 
 
-def quantise(nc, codes, scales, grouped):
-    nc.vector.quantize_mx(
-        out=codes[:].bitcast(FP8X4),
-        scales=scales[:],
-        in_=grouped[:].rearrange("p c t -> p (c t)"),
-    )
-
-
 def tile_attend_dk_kernel(tc, g, qm, offs, out):
     nc = tc.nc
     g_rows = g.rearrange("b (p t) n -> p (b t) n", t=PACK)
     qm_rows = qm.rearrange("b (p t) d -> p (b t) d", t=PACK)
-    starts = [sum(CHUNKS[:c]) for c in range(len(CHUNKS))]
-
     with ExitStack() as ctx:
         held = ctx.enter_context(tc.tile_pool(name="held", bufs=1))
         psum = ctx.enter_context(tc.psum_pool(name="psum", bufs=1))
-
         offsets = held.tile([P, SLOTS // 16], U16, name="offsets")
-        qm_raw = held.tile([P, PACK, D], F32, name="qm_raw")
-        g_raw = [held.tile([P, PACK, w], F32, name=f"g_raw{c}") for c, w in enumerate(CHUNKS)]
         warm = held.tile([P, 8], F32, name="warm")
-
-        nc.sync.dma_start(out=qm_raw[:], in_=qm_rows)
-        for c, w in enumerate(CHUNKS):
-            nc.sync.dma_start(out=g_raw[c][:], in_=g_rows[:, :, starts[c] : starts[c] + w])
-            if c == 0:
-                nc.sync.dma_start(offsets[:], offs)
-
-        windows = [held.tile([P, T], F32, name=f"window{b}") for b in range(BLOCKS)]
+        q0_raw = held.tile([P, PACK, 128], F32, name="q0_raw")
+        q0_grp = held.tile([P, 128, PACK], BF16, name="q0_grp", align_bytes=64)
+        q0_codes = held.tile([P, 128], U32, name="q0_codes", align_bytes=64)
+        q0_scales = held.tile([P, 128], U8, name="q0_scales", align_bytes=64)
+        q1_raw = held.tile([P, PACK, 128], F32, name="q1_raw")
+        q1_grp = held.tile([P, 128, PACK], BF16, name="q1_grp", align_bytes=64)
+        q1_codes = held.tile([P, 128], U32, name="q1_codes", align_bytes=64)
+        q1_scales = held.tile([P, 128], U8, name="q1_scales", align_bytes=64)
+        g0_raw = held.tile([P, PACK, 128], F32, name="g0_raw")
+        g0_grp = held.tile([P, 128, PACK], BF16, name="g0_grp", align_bytes=64)
+        g0_codes = held.tile([P, 128], U32, name="g0_codes", align_bytes=64)
+        g0_scales = held.tile([P, 128], U8, name="g0_scales", align_bytes=64)
+        g1_raw = held.tile([P, PACK, 128], F32, name="g1_raw")
+        g1_grp = held.tile([P, 128, PACK], BF16, name="g1_grp", align_bytes=64)
+        g1_codes = held.tile([P, 128], U32, name="g1_codes", align_bytes=64)
+        g1_scales = held.tile([P, 128], U8, name="g1_scales", align_bytes=64)
+        g2_raw = held.tile([P, PACK, 256], F32, tag="late", name="g2_raw")
+        g2_grp = held.tile([P, 256, PACK], BF16, name="g2_grp", align_bytes=64)
+        g2_codes = held.tile([P, 256], U32, name="g2_codes", align_bytes=64)
+        g2_scales = held.tile([P, 256], U8, name="g2_scales", align_bytes=64)
+        nc.sync.dma_start(out=q0_raw[:], in_=qm_rows[:, :, 0 : 128])
+        nc.sync.dma_start(out=g0_raw[:], in_=g_rows[:, :, 0 : 128])
+        nc.sync.dma_start(out=q1_raw[:], in_=qm_rows[:, :, 128 : 256])
+        nc.sync.dma_start(out=g1_raw[:], in_=g_rows[:, :, 128 : 256])
+        nc.sync.dma_start(offsets[:], offs)
+        nc.sync.dma_start(out=g2_raw[:], in_=g_rows[:, :, 256 : 512])
+        win0 = held.tile([P, T], F32, name="win0")
+        win1 = held.tile([P, T], F32, name="win1")
         nc.vector.memset(warm[:], 0.0)
         nc.scalar.copy(out=warm[:, 4:8], in_=warm[:, 0:4])
-        nc.vector.memset(windows[0][:], 0.0)
-        nc.gpsimd.memset(windows[1][:], 0.0)
-
-        qm_grouped = held.tile([P, D, PACK], BF16, name="qm_grouped", align_bytes=64)
-        qm_codes = held.tile([P, D], U32, name="qm_codes", align_bytes=64)
-        qm_scales = held.tile([P, D], U8, name="qm_scales", align_bytes=64)
-        interleave(nc, qm_grouped, qm_raw, 176, D)
-        quantise(nc, qm_codes, qm_scales, qm_grouped)
-
-        g_codes, g_scales, staged = [], [], []
-        for c, w in enumerate(CHUNKS):
-            grouped = held.tile([P, w, PACK], BF16, name=f"g_grouped{c}", align_bytes=64)
-            g_codes.append(held.tile([P, w], U32, name=f"g_codes{c}", align_bytes=64))
-            g_scales.append(held.tile([P, w], U8, name=f"g_scales{c}", align_bytes=64))
-            interleave(nc, grouped, g_raw[c], int(w * 0.69) // 8 * 8, w)
-            quantise(nc, g_codes[c], g_scales[c], grouped)
-
-            for b in range(BLOCKS):
-                rows = slice(b * P, (b + 1) * P)
-                acc = psum.tile([P, w], F32, name=f"acc{c}_{b}")
-                nc.tensor.matmul_mx(
-                    out=acc[:],
-                    lhsT=qm_codes[:, rows].bitcast(FP8X4),
-                    lhsT_scale=qm_scales[:, rows],
-                    rhs=g_codes[c][:].bitcast(FP8X4),
-                    rhs_scale=g_scales[c][:],
-                    start=True,
-                    stop=True,
-                )
-                values = held.tile([P, w], F32, name=f"values{c}_{b}")
-                nc.scalar.copy(out=values[:], in_=acc[:])
-                staged.append((b, c, values))
-
-        for b, c, values in sorted(staged, key=lambda s: s[0] * 10 + s[1]):
-            listed = offsets[:, starts[c] // 16 : (starts[c] + CHUNKS[c]) // 16]
-            nc.vector.tensor_copy(windows[b][:].indirect(listed), values[:])
-        for b in range(BLOCKS):
-            nc.sync.dma_start(out=out[b * P : (b + 1) * P, :], in_=windows[b][:])
+        nc.vector.memset(win0[:], 0.0)
+        nc.gpsimd.memset(win1[:], 0.0)
+        interleave(nc, q0_grp, q0_raw, 128, 128)
+        interleave(nc, g0_grp, g0_raw, 128, 128)
+        nc.vector.quantize_mx(out=q0_codes[:].bitcast(FP8X4), scales=q0_scales[:], in_=q0_grp[:].rearrange("p c t -> p (c t)"))
+        nc.vector.quantize_mx(out=g0_codes[:].bitcast(FP8X4), scales=g0_scales[:], in_=g0_grp[:].rearrange("p c t -> p (c t)"))
+        acc0_0 = psum.tile([P, 128], F32, name="acc0_0")
+        nc.tensor.matmul_mx(out=acc0_0[:], lhsT=q0_codes[:].bitcast(FP8X4), lhsT_scale=q0_scales[:], rhs=g0_codes[:].bitcast(FP8X4), rhs_scale=g0_scales[:], start=True, stop=True)
+        val0_0 = held.tile([P, 128], F32, name="val0_0")
+        nc.vector.tensor_copy(out=val0_0[:], in_=acc0_0[:])
+        interleave(nc, q1_grp, q1_raw, 0, 128)
+        nc.vector.quantize_mx(out=q1_codes[:].bitcast(FP8X4), scales=q1_scales[:], in_=q1_grp[:].rearrange("p c t -> p (c t)"))
+        acc1_0 = psum.tile([P, 128], F32, name="acc1_0")
+        nc.tensor.matmul_mx(out=acc1_0[:], lhsT=q1_codes[:].bitcast(FP8X4), lhsT_scale=q1_scales[:], rhs=g0_codes[:].bitcast(FP8X4), rhs_scale=g0_scales[:], start=True, stop=True)
+        val1_0 = held.tile([P, 128], F32, name="val1_0")
+        nc.scalar.copy(out=val1_0[:], in_=acc1_0[:])
+        interleave(nc, g1_grp, g1_raw, 128, 128)
+        nc.vector.quantize_mx(out=g1_codes[:].bitcast(FP8X4), scales=g1_scales[:], in_=g1_grp[:].rearrange("p c t -> p (c t)"))
+        acc0_1 = psum.tile([P, 128], F32, name="acc0_1")
+        nc.tensor.matmul_mx(out=acc0_1[:], lhsT=q0_codes[:].bitcast(FP8X4), lhsT_scale=q0_scales[:], rhs=g1_codes[:].bitcast(FP8X4), rhs_scale=g1_scales[:], start=True, stop=True)
+        val0_1 = held.tile([P, 128], F32, name="val0_1")
+        nc.scalar.copy(out=val0_1[:], in_=acc0_1[:])
+        interleave(nc, g2_grp, g2_raw, 0, 256)
+        nc.vector.quantize_mx(out=g2_codes[:].bitcast(FP8X4), scales=g2_scales[:], in_=g2_grp[:].rearrange("p c t -> p (c t)"))
+        acc1_1 = psum.tile([P, 128], F32, name="acc1_1")
+        nc.tensor.matmul_mx(out=acc1_1[:], lhsT=q1_codes[:].bitcast(FP8X4), lhsT_scale=q1_scales[:], rhs=g1_codes[:].bitcast(FP8X4), rhs_scale=g1_scales[:], start=True, stop=True)
+        val1_1 = held.tile([P, 128], F32, tag="late", name="val1_1")
+        nc.scalar.copy(out=val1_1[:], in_=acc1_1[:])
+        acc0_2 = psum.tile([P, 256], F32, name="acc0_2")
+        nc.tensor.matmul_mx(out=acc0_2[:], lhsT=q0_codes[:].bitcast(FP8X4), lhsT_scale=q0_scales[:], rhs=g2_codes[:].bitcast(FP8X4), rhs_scale=g2_scales[:], start=True, stop=True)
+        val0_2 = held.tile([P, 256], F32, name="val0_2")
+        nc.scalar.copy(out=val0_2[:], in_=acc0_2[:])
+        acc1_2 = psum.tile([P, 256], F32, name="acc1_2")
+        nc.tensor.matmul_mx(out=acc1_2[:], lhsT=q1_codes[:].bitcast(FP8X4), lhsT_scale=q1_scales[:], rhs=g2_codes[:].bitcast(FP8X4), rhs_scale=g2_scales[:], start=True, stop=True)
+        val1_2 = held.tile([P, 256], F32, name="val1_2")
+        nc.scalar.copy(out=val1_2[:], in_=acc1_2[:])
+        nc.vector.tensor_copy(win0[:].indirect(offsets[:, 0 : 8]), val0_0[:])
+        nc.vector.tensor_copy(win1[:].indirect(offsets[:, 0 : 8]), val1_0[:])
+        nc.vector.tensor_copy(win0[:].indirect(offsets[:, 8 : 16]), val0_1[:])
+        nc.vector.tensor_copy(win1[:].indirect(offsets[:, 8 : 16]), val1_1[:])
+        nc.vector.tensor_copy(win0[:].indirect(offsets[:, 16 : 32]), val0_2[:])
+        nc.sync.dma_start(out=out[0 : 128, :], in_=win0[:])
+        nc.vector.tensor_copy(win1[:].indirect(offsets[:, 16 : 32]), val1_2[:])
+        nc.sync.dma_start(out=out[128 : 256, :], in_=win1[:])

from contextlib import ExitStack

import concourse.mybir as mybir

F32 = mybir.dt.float32
BF16 = mybir.dt.bfloat16
U32 = mybir.dt.uint32
U16 = mybir.dt.uint16
U8 = mybir.dt.uint8
FP8X4 = mybir.dt.float8_e4m3fn_x4

P = 128
PACK = 4
NQ = 512
SLOTS = 512
D = 256
T = 1024
BLOCKS = D // P

FLOPS = 2 * NQ * SLOTS * D


CHUNKS = [128,128,256]


def interleave(nc, grouped, raw, vector_cols, width):
    for copy, a, b in ((nc.vector.tensor_copy, 0, vector_cols), (nc.scalar.copy, vector_cols, width)):
        if b > a:
            copy(
                out=grouped[:, a:b, :].rearrange("p (c i) t -> p c t i", i=4),
                in_=raw[:, :, a:b].rearrange("p t (c i) -> p c t i", i=4),
            )


def tile_attend_dk_kernel(tc, g, qm, offs, out):
    nc = tc.nc
    g_rows = g.rearrange("b (p t) n -> p (b t) n", t=PACK)
    qm_rows = qm.rearrange("b (p t) d -> p (b t) d", t=PACK)
    with ExitStack() as ctx:
        held = ctx.enter_context(tc.tile_pool(name="held", bufs=1))
        psum = ctx.enter_context(tc.psum_pool(name="psum", bufs=1))
        offsets = held.tile([P, SLOTS // 16], U16, name="offsets")
        warm = held.tile([P, 8], F32, name="warm")
        q0_raw = held.tile([P, PACK, 128], F32, name="q0_raw")
        q0_grp = held.tile([P, 128, PACK], BF16, name="q0_grp", align_bytes=64)
        q0_codes = held.tile([P, 128], U32, name="q0_codes", align_bytes=64)
        q0_scales = held.tile([P, 128], U8, name="q0_scales", align_bytes=64)
        q1_raw = held.tile([P, PACK, 128], F32, name="q1_raw")
        q1_grp = held.tile([P, 128, PACK], BF16, name="q1_grp", align_bytes=64)
        q1_codes = held.tile([P, 128], U32, name="q1_codes", align_bytes=64)
        q1_scales = held.tile([P, 128], U8, name="q1_scales", align_bytes=64)
        g0_raw = held.tile([P, PACK, 128], F32, name="g0_raw")
        g0_grp = held.tile([P, 128, PACK], BF16, name="g0_grp", align_bytes=64)
        g0_codes = held.tile([P, 128], U32, name="g0_codes", align_bytes=64)
        g0_scales = held.tile([P, 128], U8, name="g0_scales", align_bytes=64)
        g1_raw = held.tile([P, PACK, 128], F32, name="g1_raw")
        g1_grp = held.tile([P, 128, PACK], BF16, name="g1_grp", align_bytes=64)
        g1_codes = held.tile([P, 128], U32, name="g1_codes", align_bytes=64)
        g1_scales = held.tile([P, 128], U8, name="g1_scales", align_bytes=64)
        g2_raw = held.tile([P, PACK, 256], F32, tag="late", name="g2_raw")
        g2_grp = held.tile([P, 256, PACK], BF16, name="g2_grp", align_bytes=64)
        g2_codes = held.tile([P, 256], U32, name="g2_codes", align_bytes=64)
        g2_scales = held.tile([P, 256], U8, name="g2_scales", align_bytes=64)
        nc.sync.dma_start(out=q0_raw[:], in_=qm_rows[:, :, 0 : 128])
        nc.sync.dma_start(out=g0_raw[:], in_=g_rows[:, :, 0 : 128])
        nc.sync.dma_start(out=q1_raw[:], in_=qm_rows[:, :, 128 : 256])
        nc.sync.dma_start(out=g1_raw[:], in_=g_rows[:, :, 128 : 256])
        nc.sync.dma_start(offsets[:], offs)
        nc.sync.dma_start(out=g2_raw[:], in_=g_rows[:, :, 256 : 512])
        win0 = held.tile([P, T], F32, name="win0")
        win1 = held.tile([P, T], F32, name="win1")
        nc.vector.memset(warm[:], 0.0)
        nc.scalar.copy(out=warm[:, 4:8], in_=warm[:, 0:4])
        nc.vector.memset(win0[:], 0.0)
        nc.gpsimd.memset(win1[:], 0.0)
        interleave(nc, q0_grp, q0_raw, 128, 128)
        interleave(nc, g0_grp, g0_raw, 128, 128)
        nc.vector.quantize_mx(out=q0_codes[:].bitcast(FP8X4), scales=q0_scales[:], in_=q0_grp[:].rearrange("p c t -> p (c t)"))
        nc.vector.quantize_mx(out=g0_codes[:].bitcast(FP8X4), scales=g0_scales[:], in_=g0_grp[:].rearrange("p c t -> p (c t)"))
        acc0_0 = psum.tile([P, 128], F32, name="acc0_0")
        nc.tensor.matmul_mx(out=acc0_0[:], lhsT=q0_codes[:].bitcast(FP8X4), lhsT_scale=q0_scales[:], rhs=g0_codes[:].bitcast(FP8X4), rhs_scale=g0_scales[:], start=True, stop=True)
        val0_0 = held.tile([P, 128], F32, name="val0_0")
        nc.vector.tensor_copy(out=val0_0[:], in_=acc0_0[:])
        interleave(nc, q1_grp, q1_raw, 0, 128)
        nc.vector.quantize_mx(out=q1_codes[:].bitcast(FP8X4), scales=q1_scales[:], in_=q1_grp[:].rearrange("p c t -> p (c t)"))
        acc1_0 = psum.tile([P, 128], F32, name="acc1_0")
        nc.tensor.matmul_mx(out=acc1_0[:], lhsT=q1_codes[:].bitcast(FP8X4), lhsT_scale=q1_scales[:], rhs=g0_codes[:].bitcast(FP8X4), rhs_scale=g0_scales[:], start=True, stop=True)
        val1_0 = held.tile([P, 128], F32, name="val1_0")
        nc.scalar.copy(out=val1_0[:], in_=acc1_0[:])
        interleave(nc, g1_grp, g1_raw, 128, 128)
        nc.vector.quantize_mx(out=g1_codes[:].bitcast(FP8X4), scales=g1_scales[:], in_=g1_grp[:].rearrange("p c t -> p (c t)"))
        acc0_1 = psum.tile([P, 128], F32, name="acc0_1")
        nc.tensor.matmul_mx(out=acc0_1[:], lhsT=q0_codes[:].bitcast(FP8X4), lhsT_scale=q0_scales[:], rhs=g1_codes[:].bitcast(FP8X4), rhs_scale=g1_scales[:], start=True, stop=True)
        val0_1 = held.tile([P, 128], F32, name="val0_1")
        nc.scalar.copy(out=val0_1[:], in_=acc0_1[:])
        interleave(nc, g2_grp, g2_raw, 0, 256)
        nc.vector.quantize_mx(out=g2_codes[:].bitcast(FP8X4), scales=g2_scales[:], in_=g2_grp[:].rearrange("p c t -> p (c t)"))
        acc1_1 = psum.tile([P, 128], F32, name="acc1_1")
        nc.tensor.matmul_mx(out=acc1_1[:], lhsT=q1_codes[:].bitcast(FP8X4), lhsT_scale=q1_scales[:], rhs=g1_codes[:].bitcast(FP8X4), rhs_scale=g1_scales[:], start=True, stop=True)
        val1_1 = held.tile([P, 128], F32, tag="late", name="val1_1")
        nc.scalar.copy(out=val1_1[:], in_=acc1_1[:])
        acc0_2 = psum.tile([P, 256], F32, name="acc0_2")
        nc.tensor.matmul_mx(out=acc0_2[:], lhsT=q0_codes[:].bitcast(FP8X4), lhsT_scale=q0_scales[:], rhs=g2_codes[:].bitcast(FP8X4), rhs_scale=g2_scales[:], start=True, stop=True)
        val0_2 = held.tile([P, 256], F32, name="val0_2")
        nc.scalar.copy(out=val0_2[:], in_=acc0_2[:])
        acc1_2 = psum.tile([P, 256], F32, name="acc1_2")
        nc.tensor.matmul_mx(out=acc1_2[:], lhsT=q1_codes[:].bitcast(FP8X4), lhsT_scale=q1_scales[:], rhs=g2_codes[:].bitcast(FP8X4), rhs_scale=g2_scales[:], start=True, stop=True)
        val1_2 = held.tile([P, 256], F32, name="val1_2")
        nc.scalar.copy(out=val1_2[:], in_=acc1_2[:])
        nc.vector.tensor_copy(win0[:].indirect(offsets[:, 0 : 8]), val0_0[:])
        nc.vector.tensor_copy(win1[:].indirect(offsets[:, 0 : 8]), val1_0[:])
        nc.vector.tensor_copy(win0[:].indirect(offsets[:, 8 : 16]), val0_1[:])
        nc.vector.tensor_copy(win1[:].indirect(offsets[:, 8 : 16]), val1_1[:])
        nc.vector.tensor_copy(win0[:].indirect(offsets[:, 16 : 32]), val0_2[:])
        nc.sync.dma_start(out=out[0 : 128, :], in_=win0[:])
        nc.vector.tensor_copy(win1[:].indirect(offsets[:, 16 : 32]), val1_2[:])
        nc.sync.dma_start(out=out[128 : 256, :], in_=win1[:])
